import numpy as np
import ml_dtypes


def mxq(x, axis, fmt="e4m3"):
    dtype, down = {"e4m3": (ml_dtypes.float8_e4m3fn, 7), "e5m2": (ml_dtypes.float8_e5m2, 14)}[fmt]
    v = np.moveaxis(np.asarray(x, np.float32).astype(ml_dtypes.bfloat16).astype(np.float64), axis, -1)
    blocks = v.reshape(v.shape[:-1] + (-1, 32))
    amax = np.abs(blocks).max(-1, keepdims=True)
    byte = np.maximum(np.where(amax > 0, np.frexp(amax)[1] - 1 + 127, 0) - down, 1)
    scale = np.exp2(byte - 127.0)
    codes = (blocks / scale).astype(np.float32).astype(dtype).astype(np.float64)
    return np.moveaxis((codes * scale).reshape(v.shape), -1, axis)


WIDE = False


def mx_kscale(k):
    if not WIDE:
        return np.ones(k)
    levels = np.array([10, -10, 5, -5, 0])
    if k % 512:
        return np.exp2(np.random.permutation(np.resize(levels, k // 32))).repeat(32)
    a = np.empty((k // 512, 16))
    for p in range(k // 512):
        a[p, :8] = np.random.permutation(np.resize(levels, 8))
        for g in range(8):
            far = levels[np.abs(levels - a[p, g]) >= 10]
            a[p, g + 8] = far[np.random.randint(len(far))]
    return np.exp2(a.ravel()).repeat(32)


def f64(x):
    return np.asarray(x).astype(np.float64)


def striped(idx):
    return np.tile(np.asarray(idx).reshape(-1, 16).T, (8, 1)).astype(np.uint16)


def unstriped(offs):
    return offs[:16].T.reshape(-1).astype(np.int64)


E2M1 = np.array([0.0, 0.5, 1.0, 1.5, 2.0, 3.0, 4.0, 6.0, -0.0, -0.5, -1.0, -1.5, -2.0, -3.0, -4.0, -6.0])


def pack_weight(w, fmt):
    k, n = w.shape
    w = f64(np.asarray(w, np.float32).astype(ml_dtypes.bfloat16)).reshape(k // 32, 32, n)
    amax = np.abs(w).max(1)
    if fmt == "e4m3":
        byte = np.frexp(amax)[1] - 1 + 127 - 7
    else:
        mant, ex = np.frexp(amax / 6.0)
        byte = np.where(mant > 0.5, ex, ex - 1) + 127
    byte = np.clip(np.where(amax > 0, byte, 1), 1, 254)
    scaled = (w * np.exp2(127.0 - byte)[:, None, :]).reshape(k, n).astype(np.float32)
    by_word = np.ascontiguousarray(scaled.reshape(k // 512, 128, 4, n).transpose(0, 1, 3, 2))
    if fmt == "e4m3":
        words = by_word.astype(ml_dtypes.float8_e4m3fn).view(np.uint8)
    else:
        c = by_word.astype(ml_dtypes.float4_e2m1fn).view(np.uint8) & 0xF
        words = (c[..., 0::2] | (c[..., 1::2] << 4)).reshape(k // 512, 128, 2 * n)
    return np.ascontiguousarray(words), np.ascontiguousarray(byte.astype(np.uint8).reshape(k // 512, 16, n))


def unpack_weight(words, scales, fmt):
    g, _, n = scales.shape
    words = np.ascontiguousarray(words).reshape(g, 128, n, -1)
    if fmt == "e4m3":
        vals = words.view(ml_dtypes.float8_e4m3fn).astype(np.float64)
    else:
        nib = np.empty((g, 128, n, 4), np.uint8)
        nib[..., 0::2] = words & 0xF
        nib[..., 1::2] = words >> 4
        vals = E2M1[nib]
    vals = vals * np.repeat(np.exp2(scales.astype(np.float64) - 127.0), 8, axis=1)[..., None]
    return vals.transpose(0, 1, 3, 2).reshape(g * 512, n)


B, N, T, D, DV, NQ = 2, 512, 2048, 512, 256, 256


def setup_inputs():
    n = np.random.standard_normal
    seg = T // B
    idx = np.concatenate([b * seg + np.random.permutation(seg)[:N] for b in range(B)])
    s = mx_kscale(D)[:, None]
    u = np.ones(T)
    u[idx] = mx_kscale(B * N)
    r = np.random.uniform(0.5, 2.0, T)
    k = n((D, T)) / s
    v = n((DV, T)) / (u * r)
    kp = pack_weight(k, "e4m3")
    return {
        "qT": (n((B, D, NQ)) * s * (0.80 / np.sqrt(D))).astype(np.float32),
        "k_words": kp[0],
        "k_scales": kp[1],
        "vT": v.astype(np.float32),
        "vs": np.tile(u * r, (128, 1)).astype(np.float32),
        "kb": np.tile(n(T), (128, 1)).astype(np.float32),
        "og": n((B, NQ, DV)).astype(np.float32),
        "offs": striped(idx),
    }


def reference(qT, k_words, k_scales, vT, vs, kb, og, offs):
    idx = unstriped(offs)
    k = unpack_weight(k_words, k_scales, "e4m3")
    v = f64(vT)
    pick = lambda x: x[:, idx].reshape(x.shape[0], B, N).transpose(1, 0, 2)
    q = f64(qT)
    score = mxq(q, 1, "e4m3").transpose(0, 2, 1) @ pick(k)
    score = score + pick(f64(kb))[:, :1, :]
    p = np.square(np.maximum(score, 0.0))
    total = p.sum(-1, keepdims=True) + 1.0
    w = p * pick(f64(vs))[:, :1, :]
    y = mxq(w, 2, "e4m3") @ mxq(pick(v).transpose(0, 2, 1), 1, "e4m3")
    y = y / total
    y = y / (1.0 + np.exp(-f64(og)))
    return y

@@ -1,0 +1,301 @@
+from contextlib import ExitStack
+
+import concourse.mybir as mybir
+from concourse.masks import make_identity
+
+B, N, T, D, DV, NQ = 2, 512, 2048, 512, 256, 256
+SEG = T // B
+FLOPS = 2 * B * NQ * N * (D + DV)
+BYTES = 4 * (B * D * NQ + DV * T + 2 * T + 2 * B * NQ * DV) + D * T + 16 * T + 2 * 128 * 64
+
+F32 = mybir.dt.float32
+BF16 = mybir.dt.bfloat16
+I32 = mybir.dt.int32
+U32 = mybir.dt.uint32
+U16 = mybir.dt.uint16
+U8 = mybir.dt.uint8
+FP8X4 = mybir.dt.float8_e4m3fn_x4
+ALU = mybir.AluOpType
+ACT = mybir.ActivationFunctionType
+
+P = 128
+PACK = 4
+COLS = N // 16
+
+
+def tile_attend_rel2_kb_gate_segb2q256n512t2048_kernel(tc, qT, k_words, k_scales, vT, vs, kb, og, offs, out):
+    nc = tc.nc
+    with ExitStack() as ctx:
+        keep = ctx.enter_context(tc.tile_pool(name="keep", bufs=1))
+        psum = ctx.enter_context(tc.psum_pool(name="psum", bufs=1))
+
+        def sb(name, shape, dt):
+            return keep.tile(shape, dt, name=name, align_bytes=64)
+
+        offsets = sb("offsets", [P, B * COLS], U16)
+        nc.sync.dma_start(offsets[:], offs)
+
+        ks_win = sb("ks_win", [P, T], U8)
+        rows = {"kb": sb("kb_win", [P, T], F32), "vs": sb("vs_win", [P, T], F32)}
+        row_dram = {"kb": kb, "vs": vs}
+        kw_win = sb("kw_win", [P, T], I32)
+        v_raw = [sb(f"v_raw{j}", [P, T], F32) for j in range(2)]
+        v_cast = [sb(f"v_cast{j}", [P, SEG], BF16) for j in range(2)]
+        ident = sb("ident", [P, P], F32)
+        warm = sb("warm", [P, 8], F32)
+        q_raw = [sb(f"q_raw{b}", [P, PACK, NQ], F32) for b in range(B)]
+        og_raw = sb("og_raw", [P, B * 2, DV], F32)
+        gate = sb("gate", [P, B * 2, DV], F32)
+        v_g = [sb(f"v_g{b}", [P, 2, N], BF16) for b in range(B)]
+
+        def seg(b):
+            return slice(b * SEG, (b + 1) * SEG)
+
+        for b in range(B):
+            for name in ("kb", "vs"):
+                nc.vector.memset(rows[name][:, seg(b)], 0.0)
+        make_identity(nc, ident[:])
+        nc.scalar.activation(warm[:], ident[:, 0:8], ACT.Sigmoid)
+
+        ks_rows = k_scales[0].rearrange("(a r) t -> a (r t)", r=4).bitcast(I32)
+        for quad in range(4):
+            nc.sync.dma_start(
+                ks_win[32 * quad : 32 * quad + 32, :].bitcast(I32), ks_rows[quad : quad + 1, :].to_broadcast([8, T])
+            )
+        kw_dram = k_words[0].rearrange("p t r -> p (t r)").bitcast(I32)
+
+        def load_v(b, j):
+            nc.sync.dma_start(v_raw[j][:, seg(b)], vT[j * P : (j + 1) * P, seg(b)])
+
+        def load_q(b):
+            nc.sync.dma_start(q_raw[b][:], qT[b].rearrange("(p j) q -> p j q", j=PACK))
+
+        def load_k(b):
+            nc.sync.dma_start(kw_win[:, seg(b)], kw_dram[:, seg(b)])
+
+        def load_row(name, b):
+            nc.sync.dma_start(rows[name][0:1, seg(b)], row_dram[name][0:1, seg(b)])
+
+        def load_og():
+            nc.sync.dma_start(og_raw[:], og.rearrange("b (h p) e -> p (b h) e", p=P))
+
+        def window(ap, b):
+            return ap[:, 0 : (b + 1) * SEG].indirect(offsets[:, b * COLS : (b + 1) * COLS])
+
+        def quantize(name, src):
+            width = src.shape[1]
+            codes = sb(name + "_codes", [P, width], U32)
+            scales = sb(name + "_scales", [P, width], U8)
+            nc.vector.quantize_mx(out=codes[:].bitcast(FP8X4), scales=scales[:], in_=src.rearrange("p c t -> p (c t)"))
+            return codes, scales
+
+        def turn_bank(name):
+            return psum.tile([P, PACK, P], F32, name=name, tag="turn", bufs=4)
+
+        st = [dict() for b in range(B)]
+
+        def key_scales(b):
+            s = st[b]
+            s["ks_g"] = sb(f"ks_g{b}", [P, N], U8)
+            nc.vector.tensor_copy(s["ks_g"][:], window(ks_win[:], b))
+
+        def turn_scales(b):
+            s = st[b]
+            s["ks"] = sb(f"ks{b}", [P, N], U8)
+            nc.vector.tensor_copy(
+                s["ks"][:].rearrange("p (t m) -> p t m", t=PACK), s["ks_g"][:].rearrange("p (m t) -> p t m", t=PACK)
+            )
+
+        def key_words(b):
+            s = st[b]
+            s["kw"] = sb(f"kw_g{b}", [P, N], U32)
+            nc.vector.tensor_copy(
+                s["kw"][:].rearrange("p (t m) -> p m t", t=PACK), window(kw_win[:].bitcast(U32), b)
+            )
+
+        def token_row(name, b):
+            g = sb(f"{name}_g{b}", [P, N], F32)
+            nc.vector.tensor_copy(g[:], window(rows[name][:], b))
+            bank = turn_bank(f"{name}_ps{b}")
+            for t in range(PACK):
+                nc.tensor.transpose(bank[:, t, :], g[:, t:N:PACK], ident[:])
+            st[b][name] = bank[:, :, 0]
+
+        def to_column(name, b):
+            col = sb(f"{name}_col{b}", [P, PACK], F32)
+            nc.scalar.activation(col[:], st[b][name], ACT.Copy)
+            st[b][name] = col[:]
+
+        def cast_q(b):
+            q_bf = sb(f"q_bf{b}", [P, NQ, PACK], BF16)
+            nc.scalar.activation(
+                q_bf[:].rearrange("p (c i) t -> p c t i", i=4),
+                q_raw[b][:].rearrange("p t (c i) -> p c t i", i=4),
+                ACT.Copy,
+            )
+            st[b]["q_bf"] = q_bf
+
+        def scores(b):
+            s = st[b]
+            q_codes, q_scales = quantize(f"q{b}", s["q_bf"][:])
+            s["r"] = sb(f"r{b}", [P, PACK, NQ], F32)
+            s["p"] = sb(f"p{b}", [P, PACK, NQ], F32)
+            for u in range(2):
+                bank = psum.tile([P, 2, NQ], F32, name=f"sc{b}{u}", tag="score", bufs=2)
+                for tt in range(2):
+                    cols = slice((2 * u + tt) * P, (2 * u + tt + 1) * P)
+                    nc.tensor.matmul_mx(
+                        out=bank[:, tt, :],
+                        lhsT=s["kw"][:, cols].bitcast(FP8X4),
+                        lhsT_scale=s["ks"][:, cols],
+                        rhs=q_codes[:].bitcast(FP8X4),
+                        rhs_scale=q_scales[:],
+                        start=True,
+                        stop=True,
+                    )
+                for tt in range(2):
+                    t = 2 * u + tt
+                    nc.scalar.activation(s["r"][:, t, :], bank[:, tt, :], ACT.Relu, bias=s["kb"][:, t : t + 1])
+                nc.scalar.activation(s["p"][:, 2 * u : 2 * u + 2, :], s["r"][:, 2 * u : 2 * u + 2, :], ACT.Square)
+
+        def cast_v(b, j, engine):
+            if engine == "scalar":
+                nc.scalar.activation(v_cast[j][:, seg(b)], v_raw[j][:, seg(b)], ACT.Copy)
+            else:
+                nc.vector.tensor_copy(v_cast[j][:, seg(b)], v_raw[j][:, seg(b)])
+
+        def gather_v(b, j, engine):
+            dst = v_g[b][:, j, :].rearrange("p (u m i) -> p m u i", u=2, i=2)
+            if engine == "scalar":
+                nc.scalar.activation(dst, window(v_cast[j][:], b), ACT.Copy)
+            else:
+                nc.vector.tensor_copy(dst, window(v_raw[j][:], b))
+
+        def values(b):
+            s = st[b]
+            words = v_g[b][:].rearrange("p j n -> p (j n)").bitcast(F32)
+            bank = turn_bank(f"v_ps{b}")
+            for j in range(2):
+                for u in range(2):
+                    c = (2 * j + u) * P
+                    nc.tensor.transpose(bank[:, 2 * u + j, :], words[:, c : c + P], ident[:])
+            s["v_bf"] = sb(f"v_bf{b}", [P, DV, PACK], BF16)
+            nc.scalar.copy(
+                s["v_bf"][:].rearrange("p e t -> p (e t)").bitcast(F32).rearrange("p (e u) -> p e u", u=2),
+                bank[:].rearrange("p (u j) w -> p (j w) u", u=2),
+            )
+
+        def row_sums(b):
+            s = st[b]
+            bank = turn_bank(f"l_ps{b}")
+            total = sb(f"total{b}", [P, 2], F32)
+            junk = sb(f"junk{b}", [P, 2, 2 * P], F32)
+            for u in range(2):
+                for h in range(2):
+                    for tt in range(2):
+                        nc.tensor.matmul(
+                            bank[:, 2 * h + u, :], s["p"][:, 2 * u + tt, h * P : (h + 1) * P], ident[:],
+                            start=(tt == 0), stop=(tt == 1), is_transpose=True,
+                        )
+            for h in range(2):
+                nc.scalar.activation(
+                    junk[:, h, :], bank[:, 2 * h : 2 * h + 2, :].rearrange("p u m -> p (u m)"), ACT.Copy,
+                    bias=1.0 / (2 * P), accum_out=total[:, h : h + 1],
+                )
+            s["rl"] = sb(f"rl{b}", [P, 2], F32)
+            nc.vector.reciprocal(s["rl"][:], total[:])
+
+        def weights(b):
+            s = st[b]
+            s["w_bf"] = sb(f"w_bf{b}", [P, NQ, PACK], BF16)
+            nc.vector.tensor_tensor(
+                s["w_bf"][:].rearrange("p (c i) t -> p c t i", i=4),
+                s["p"][:].rearrange("p t (c i) -> p c t i", i=4),
+                s["vs"].unsqueeze(1).unsqueeze(3).to_broadcast([P, NQ // 4, PACK, 4]),
+                ALU.mult,
+            )
+
+        def quant_v(b):
+            st[b]["vq"] = quantize(f"v{b}", st[b]["v_bf"][:])
+
+        def quant_w(b):
+            st[b]["wq"] = quantize(f"w{b}", st[b]["w_bf"][:])
+
+        def mix(b):
+            s = st[b]
+            v_codes, v_scales = s["vq"]
+            w_codes, w_scales = s["wq"]
+            s["y"] = psum.tile([P, 2, DV], F32, name=f"y_ps{b}", tag="y", bufs=2)
+            for h in range(2):
+                cols = slice(h * P, (h + 1) * P)
+                nc.tensor.matmul_mx(
+                    out=s["y"][:, h, :],
+                    lhsT=w_codes[:, cols].bitcast(FP8X4),
+                    lhsT_scale=w_scales[:, cols],
+                    rhs=v_codes[:].bitcast(FP8X4),
+                    rhs_scale=v_scales[:],
+                    start=True,
+                    stop=True,
+                )
+
+        def finish(b):
+            s = st[b]
+            res = sb(f"res{b}", [P, 2, DV], F32)
+            for h in range(2):
+                nc.vector.scalar_tensor_tensor(
+                    res[:, h, :], s["y"][:, h, :], s["rl"][:, h : h + 1], gate[:, 2 * b + h, :], ALU.mult, ALU.mult
+                )
+                nc.sync.dma_start(out[b, h * P : (h + 1) * P, :], res[:, h, :])
+
+        load_v(0, 1)
+        load_row("kb", 0)
+        cast_v(0, 1, "scalar")
+        token_row("kb", 0)
+        load_q(0)
+        load_k(0)
+        load_og()
+        key_scales(1)
+        to_column("kb", 0)
+        load_q(1)
+        key_scales(0)
+        load_row("vs", 0)
+        cast_q(0)
+        load_row("vs", 1)
+        gather_v(0, 1, "scalar")
+        key_words(0)
+        turn_scales(0)
+        load_row("kb", 1)
+        load_v(1, 1)
+        scores(0)
+        token_row("vs", 0)
+        token_row("kb", 1)
+        load_v(1, 0)
+        load_v(0, 0)
+        cast_q(1)
+        cast_v(0, 0, "scalar")
+        token_row("vs", 1)
+        turn_scales(1)
+        to_column("kb", 1)
+        load_k(1)
+        to_column("vs", 1)
+        key_words(1)
+        gather_v(0, 0, "scalar")
+        scores(1)
+        gather_v(1, 0, "vector")
+        gather_v(1, 1, "vector")
+        to_column("vs", 0)
+        weights(1)
+        values(0)
+        values(1)
+        quant_w(1)
+        weights(0)
+        quant_v(0)
+        quant_v(1)
+        row_sums(0)
+        nc.scalar.activation(gate[:], og_raw[:], ACT.Sigmoid)
+        row_sums(1)
+        quant_w(0)
+        mix(0)
+        mix(1)
+        finish(1)
+        finish(0)

@@ -37,12 +37,11 @@ def tile_attend_rel2_kb_gate_segb2q256n512t2048_kernel(tc, qT, k_words, k_scales
 
         ks_win = sb("ks_win", [P, T], U8)
         rows = {"kb": sb("kb_win", [P, T], F32), "vs": sb("vs_win", [P, T], F32)}
-        row_dram = {"kb": kb, "vs": vs}
         kw_win = sb("kw_win", [P, T], I32)
         v_raw = [sb(f"v_raw{j}", [P, T], F32) for j in range(2)]
         v_cast = [sb(f"v_cast{j}", [P, SEG], BF16) for j in range(2)]
         ident = sb("ident", [P, P], F32)
-        warm = sb("warm", [P, 8], F32)
+        warm = sb("warm", [32, 8], F32)
         q_raw = [sb(f"q_raw{b}", [P, PACK, NQ], F32) for b in range(B)]
         og_raw = sb("og_raw", [P, B * 2, DV], F32)
         gate = sb("gate", [P, B * 2, DV], F32)
@@ -51,17 +50,12 @@ def tile_attend_rel2_kb_gate_segb2q256n512t2048_kernel(tc, qT, k_words, k_scales
         def seg(b):
             return slice(b * SEG, (b + 1) * SEG)
 
-        for b in range(B):
-            for name in ("kb", "vs"):
-                nc.vector.memset(rows[name][:, seg(b)], 0.0)
+        nc.vector.memset(ks_win[:].bitcast(I32), 0)
+        nc.vector.memset(rows["kb"][0 : P - 1, :], 0.0)
+        nc.sync.dma_start(rows["kb"][P - 1 : P, :], kb[0:1, :])
         make_identity(nc, ident[:])
-        nc.scalar.activation(warm[:], ident[:, 0:8], ACT.Sigmoid)
-
-        ks_rows = k_scales[0].rearrange("(a r) t -> a (r t)", r=4).bitcast(I32)
-        for quad in range(4):
-            nc.sync.dma_start(
-                ks_win[32 * quad : 32 * quad + 32, :].bitcast(I32), ks_rows[quad : quad + 1, :].to_broadcast([8, T])
-            )
+        nc.scalar.activation(warm[:], rows["kb"][0:32, 0:8], ACT.Sigmoid)
+        nc.gpsimd.memset(rows["vs"][0 : P - 1, :], 0.0)
         kw_dram = k_words[0].rearrange("p t r -> p (t r)").bitcast(I32)
 
         def load_v(b, j):
@@ -73,11 +67,15 @@ def tile_attend_rel2_kb_gate_segb2q256n512t2048_kernel(tc, qT, k_words, k_scales
         def load_k(b):
             nc.sync.dma_start(kw_win[:, seg(b)], kw_dram[:, seg(b)])
 
-        def load_row(name, b):
-            nc.sync.dma_start(rows[name][0:1, seg(b)], row_dram[name][0:1, seg(b)])
-
         def load_og():
             nc.sync.dma_start(og_raw[:], og.rearrange("b (h p) e -> p (b h) e", p=P))
+
+        load_v(0, 0)
+        for quad in range(4):
+            nc.sync.dma_start(
+                ks_win[32 * quad : 32 * quad + 4, :].bitcast(I32),
+                k_scales[0, 4 * quad : 4 * quad + 4, :].bitcast(I32),
+            )
 
         def window(ap, b):
             return ap[:, 0 : (b + 1) * SEG].indirect(offsets[:, b * COLS : (b + 1) * COLS])
@@ -119,7 +117,7 @@ def tile_attend_rel2_kb_gate_segb2q256n512t2048_kernel(tc, qT, k_words, k_scales
             bank = turn_bank(f"{name}_ps{b}")
             for t in range(PACK):
                 nc.tensor.transpose(bank[:, t, :], g[:, t:N:PACK], ident[:])
-            st[b][name] = bank[:, :, 0]
+            st[b][name] = bank[:, :, P - 1]
 
         def to_column(name, b):
             col = sb(f"{name}_col{b}", [P, PACK], F32)
@@ -248,54 +246,50 @@ def tile_attend_rel2_kb_gate_segb2q256n512t2048_kernel(tc, qT, k_words, k_scales
                 nc.sync.dma_start(out[b, h * P : (h + 1) * P, :], res[:, h, :])
 
         load_v(0, 1)
-        load_row("kb", 0)
-        cast_v(0, 1, "scalar")
-        token_row("kb", 0)
         load_q(0)
-        load_k(0)
-        load_og()
-        key_scales(1)
-        to_column("kb", 0)
-        load_q(1)
-        key_scales(0)
-        load_row("vs", 0)
-        cast_q(0)
-        load_row("vs", 1)
-        gather_v(0, 1, "scalar")
-        key_words(0)
-        turn_scales(0)
-        load_row("kb", 1)
-        load_v(1, 1)
-        scores(0)
-        token_row("vs", 0)
-        token_row("kb", 1)
-        load_v(1, 0)
-        load_v(0, 0)
-        cast_q(1)
+        nc.sync.dma_start(rows["vs"][P - 1 : P, :], vs[0:1, :])
         cast_v(0, 0, "scalar")
-        token_row("vs", 1)
-        turn_scales(1)
-        to_column("kb", 1)
+        load_q(1)
+        key_scales(1)
+        cast_q(1)
+        cast_v(0, 1, "scalar")
+        load_k(0)
+        gather_v(0, 1, "scalar")
         load_k(1)
-        to_column("vs", 1)
+        key_words(0)
+        token_row("kb", 1)
+        token_row("kb", 0)
+        load_v(1, 1)
+        to_column("kb", 1)
+        to_column("kb", 0)
+        load_og()
+        turn_scales(1)
         key_words(1)
-        gather_v(0, 0, "scalar")
-        scores(1)
+        key_scales(0)
+        token_row("vs", 1)
+        cast_q(0)
+        turn_scales(0)
+        token_row("vs", 0)
+        load_v(1, 0)
         gather_v(1, 0, "vector")
-        gather_v(1, 1, "vector")
         to_column("vs", 0)
-        weights(1)
-        values(0)
-        values(1)
-        quant_w(1)
+        scores(0)
+        to_column("vs", 1)
         weights(0)
-        quant_v(0)
-        quant_v(1)
-        row_sums(0)
-        nc.scalar.activation(gate[:], og_raw[:], ACT.Sigmoid)
-        row_sums(1)
         quant_w(0)
+        scores(1)
+        gather_v(0, 0, "scalar")
+        gather_v(1, 1, "vector")
+        values(0)
+        weights(1)
+        quant_v(0)
+        row_sums(0)
+        values(1)
+        nc.scalar.activation(gate[:], og_raw[:], ACT.Sigmoid)
         mix(0)
+        finish(0)
+        quant_v(1)
+        quant_w(1)
+        row_sums(1)
         mix(1)
         finish(1)
-        finish(0)

from contextlib import ExitStack

import concourse.mybir as mybir
from concourse.masks import make_identity

B, N, T, D, DV, NQ = 2, 512, 2048, 512, 256, 256
SEG = T // B
FLOPS = 2 * B * NQ * N * (D + DV)
BYTES = 4 * (B * D * NQ + DV * T + 2 * T + 2 * B * NQ * DV) + D * T + 16 * T + 2 * 128 * 64

F32 = mybir.dt.float32
BF16 = mybir.dt.bfloat16
I32 = mybir.dt.int32
U32 = mybir.dt.uint32
U16 = mybir.dt.uint16
U8 = mybir.dt.uint8
FP8X4 = mybir.dt.float8_e4m3fn_x4
ALU = mybir.AluOpType
ACT = mybir.ActivationFunctionType

P = 128
PACK = 4
COLS = N // 16


def tile_attend_rel2_kb_gate_segb2q256n512t2048_kernel(tc, qT, k_words, k_scales, vT, vs, kb, og, offs, out):
    nc = tc.nc
    with ExitStack() as ctx:
        keep = ctx.enter_context(tc.tile_pool(name="keep", bufs=1))
        psum = ctx.enter_context(tc.psum_pool(name="psum", bufs=1))

        def sb(name, shape, dt):
            return keep.tile(shape, dt, name=name, align_bytes=64)

        offsets = sb("offsets", [P, B * COLS], U16)
        nc.sync.dma_start(offsets[:], offs)

        ks_win = sb("ks_win", [P, T], U8)
        rows = {"kb": sb("kb_win", [P, T], F32), "vs": sb("vs_win", [P, T], F32)}
        kw_win = sb("kw_win", [P, T], I32)
        v_raw = [sb(f"v_raw{j}", [P, T], F32) for j in range(2)]
        v_cast = [sb(f"v_cast{j}", [P, SEG], BF16) for j in range(2)]
        ident = sb("ident", [P, P], F32)
        warm = sb("warm", [32, 8], F32)
        q_raw = [sb(f"q_raw{b}", [P, PACK, NQ], F32) for b in range(B)]
        og_raw = sb("og_raw", [P, B * 2, DV], F32)
        gate = sb("gate", [P, B * 2, DV], F32)
        v_g = [sb(f"v_g{b}", [P, 2, N], BF16) for b in range(B)]

        def seg(b):
            return slice(b * SEG, (b + 1) * SEG)

        nc.vector.memset(ks_win[:].bitcast(I32), 0)
        nc.vector.memset(rows["kb"][0 : P - 1, :], 0.0)
        nc.sync.dma_start(rows["kb"][P - 1 : P, :], kb[0:1, :])
        make_identity(nc, ident[:])
        nc.scalar.activation(warm[:], rows["kb"][0:32, 0:8], ACT.Sigmoid)
        nc.gpsimd.memset(rows["vs"][0 : P - 1, :], 0.0)
        kw_dram = k_words[0].rearrange("p t r -> p (t r)").bitcast(I32)

        def load_v(b, j):
            nc.sync.dma_start(v_raw[j][:, seg(b)], vT[j * P : (j + 1) * P, seg(b)])

        def load_q(b):
            nc.sync.dma_start(q_raw[b][:], qT[b].rearrange("(p j) q -> p j q", j=PACK))

        def load_k(b):
            nc.sync.dma_start(kw_win[:, seg(b)], kw_dram[:, seg(b)])

        def load_og():
            nc.sync.dma_start(og_raw[:], og.rearrange("b (h p) e -> p (b h) e", p=P))

        load_v(0, 0)
        for quad in range(4):
            nc.sync.dma_start(
                ks_win[32 * quad : 32 * quad + 4, :].bitcast(I32),
                k_scales[0, 4 * quad : 4 * quad + 4, :].bitcast(I32),
            )

        def window(ap, b):
            return ap[:, 0 : (b + 1) * SEG].indirect(offsets[:, b * COLS : (b + 1) * COLS])

        def quantize(name, src):
            width = src.shape[1]
            codes = sb(name + "_codes", [P, width], U32)
            scales = sb(name + "_scales", [P, width], U8)
            nc.vector.quantize_mx(out=codes[:].bitcast(FP8X4), scales=scales[:], in_=src.rearrange("p c t -> p (c t)"))
            return codes, scales

        def turn_bank(name):
            return psum.tile([P, PACK, P], F32, name=name, tag="turn", bufs=4)

        st = [dict() for b in range(B)]

        def key_scales(b):
            s = st[b]
            s["ks_g"] = sb(f"ks_g{b}", [P, N], U8)
            nc.vector.tensor_copy(s["ks_g"][:], window(ks_win[:], b))

        def turn_scales(b):
            s = st[b]
            s["ks"] = sb(f"ks{b}", [P, N], U8)
            nc.vector.tensor_copy(
                s["ks"][:].rearrange("p (t m) -> p t m", t=PACK), s["ks_g"][:].rearrange("p (m t) -> p t m", t=PACK)
            )

        def key_words(b):
            s = st[b]
            s["kw"] = sb(f"kw_g{b}", [P, N], U32)
            nc.vector.tensor_copy(
                s["kw"][:].rearrange("p (t m) -> p m t", t=PACK), window(kw_win[:].bitcast(U32), b)
            )

        def token_row(name, b):
            g = sb(f"{name}_g{b}", [P, N], F32)
            nc.vector.tensor_copy(g[:], window(rows[name][:], b))
            bank = turn_bank(f"{name}_ps{b}")
            for t in range(PACK):
                nc.tensor.transpose(bank[:, t, :], g[:, t:N:PACK], ident[:])
            st[b][name] = bank[:, :, P - 1]

        def to_column(name, b):
            col = sb(f"{name}_col{b}", [P, PACK], F32)
            nc.scalar.activation(col[:], st[b][name], ACT.Copy)
            st[b][name] = col[:]

        def cast_q(b):
            q_bf = sb(f"q_bf{b}", [P, NQ, PACK], BF16)
            nc.scalar.activation(
                q_bf[:].rearrange("p (c i) t -> p c t i", i=4),
                q_raw[b][:].rearrange("p t (c i) -> p c t i", i=4),
                ACT.Copy,
            )
            st[b]["q_bf"] = q_bf

        def scores(b):
            s = st[b]
            q_codes, q_scales = quantize(f"q{b}", s["q_bf"][:])
            s["r"] = sb(f"r{b}", [P, PACK, NQ], F32)
            s["p"] = sb(f"p{b}", [P, PACK, NQ], F32)
            for u in range(2):
                bank = psum.tile([P, 2, NQ], F32, name=f"sc{b}{u}", tag="score", bufs=2)
                for tt in range(2):
                    cols = slice((2 * u + tt) * P, (2 * u + tt + 1) * P)
                    nc.tensor.matmul_mx(
                        out=bank[:, tt, :],
                        lhsT=s["kw"][:, cols].bitcast(FP8X4),
                        lhsT_scale=s["ks"][:, cols],
                        rhs=q_codes[:].bitcast(FP8X4),
                        rhs_scale=q_scales[:],
                        start=True,
                        stop=True,
                    )
                for tt in range(2):
                    t = 2 * u + tt
                    nc.scalar.activation(s["r"][:, t, :], bank[:, tt, :], ACT.Relu, bias=s["kb"][:, t : t + 1])
                nc.scalar.activation(s["p"][:, 2 * u : 2 * u + 2, :], s["r"][:, 2 * u : 2 * u + 2, :], ACT.Square)

        def cast_v(b, j, engine):
            if engine == "scalar":
                nc.scalar.activation(v_cast[j][:, seg(b)], v_raw[j][:, seg(b)], ACT.Copy)
            else:
                nc.vector.tensor_copy(v_cast[j][:, seg(b)], v_raw[j][:, seg(b)])

        def gather_v(b, j, engine):
            dst = v_g[b][:, j, :].rearrange("p (u m i) -> p m u i", u=2, i=2)
            if engine == "scalar":
                nc.scalar.activation(dst, window(v_cast[j][:], b), ACT.Copy)
            else:
                nc.vector.tensor_copy(dst, window(v_raw[j][:], b))

        def values(b):
            s = st[b]
            words = v_g[b][:].rearrange("p j n -> p (j n)").bitcast(F32)
            bank = turn_bank(f"v_ps{b}")
            for j in range(2):
                for u in range(2):
                    c = (2 * j + u) * P
                    nc.tensor.transpose(bank[:, 2 * u + j, :], words[:, c : c + P], ident[:])
            s["v_bf"] = sb(f"v_bf{b}", [P, DV, PACK], BF16)
            nc.scalar.copy(
                s["v_bf"][:].rearrange("p e t -> p (e t)").bitcast(F32).rearrange("p (e u) -> p e u", u=2),
                bank[:].rearrange("p (u j) w -> p (j w) u", u=2),
            )

        def row_sums(b):
            s = st[b]
            bank = turn_bank(f"l_ps{b}")
            total = sb(f"total{b}", [P, 2], F32)
            junk = sb(f"junk{b}", [P, 2, 2 * P], F32)
            for u in range(2):
                for h in range(2):
                    for tt in range(2):
                        nc.tensor.matmul(
                            bank[:, 2 * h + u, :], s["p"][:, 2 * u + tt, h * P : (h + 1) * P], ident[:],
                            start=(tt == 0), stop=(tt == 1), is_transpose=True,
                        )
            for h in range(2):
                nc.scalar.activation(
                    junk[:, h, :], bank[:, 2 * h : 2 * h + 2, :].rearrange("p u m -> p (u m)"), ACT.Copy,
                    bias=1.0 / (2 * P), accum_out=total[:, h : h + 1],
                )
            s["rl"] = sb(f"rl{b}", [P, 2], F32)
            nc.vector.reciprocal(s["rl"][:], total[:])

        def weights(b):
            s = st[b]
            s["w_bf"] = sb(f"w_bf{b}", [P, NQ, PACK], BF16)
            nc.vector.tensor_tensor(
                s["w_bf"][:].rearrange("p (c i) t -> p c t i", i=4),
                s["p"][:].rearrange("p t (c i) -> p c t i", i=4),
                s["vs"].unsqueeze(1).unsqueeze(3).to_broadcast([P, NQ // 4, PACK, 4]),
                ALU.mult,
            )

        def quant_v(b):
            st[b]["vq"] = quantize(f"v{b}", st[b]["v_bf"][:])

        def quant_w(b):
            st[b]["wq"] = quantize(f"w{b}", st[b]["w_bf"][:])

        def mix(b):
            s = st[b]
            v_codes, v_scales = s["vq"]
            w_codes, w_scales = s["wq"]
            s["y"] = psum.tile([P, 2, DV], F32, name=f"y_ps{b}", tag="y", bufs=2)
            for h in range(2):
                cols = slice(h * P, (h + 1) * P)
                nc.tensor.matmul_mx(
                    out=s["y"][:, h, :],
                    lhsT=w_codes[:, cols].bitcast(FP8X4),
                    lhsT_scale=w_scales[:, cols],
                    rhs=v_codes[:].bitcast(FP8X4),
                    rhs_scale=v_scales[:],
                    start=True,
                    stop=True,
                )

        def finish(b):
            s = st[b]
            res = sb(f"res{b}", [P, 2, DV], F32)
            for h in range(2):
                nc.vector.scalar_tensor_tensor(
                    res[:, h, :], s["y"][:, h, :], s["rl"][:, h : h + 1], gate[:, 2 * b + h, :], ALU.mult, ALU.mult
                )
                nc.sync.dma_start(out[b, h * P : (h + 1) * P, :], res[:, h, :])

        load_v(0, 1)
        load_q(0)
        nc.sync.dma_start(rows["vs"][P - 1 : P, :], vs[0:1, :])
        cast_v(0, 0, "scalar")
        load_q(1)
        key_scales(1)
        cast_q(1)
        cast_v(0, 1, "scalar")
        load_k(0)
        gather_v(0, 1, "scalar")
        load_k(1)
        key_words(0)
        token_row("kb", 1)
        token_row("kb", 0)
        load_v(1, 1)
        to_column("kb", 1)
        to_column("kb", 0)
        load_og()
        turn_scales(1)
        key_words(1)
        key_scales(0)
        token_row("vs", 1)
        cast_q(0)
        turn_scales(0)
        token_row("vs", 0)
        load_v(1, 0)
        gather_v(1, 0, "vector")
        to_column("vs", 0)
        scores(0)
        to_column("vs", 1)
        weights(0)
        quant_w(0)
        scores(1)
        gather_v(0, 0, "scalar")
        gather_v(1, 1, "vector")
        values(0)
        weights(1)
        quant_v(0)
        row_sums(0)
        values(1)
        nc.scalar.activation(gate[:], og_raw[:], ACT.Sigmoid)
        mix(0)
        finish(0)
        quant_v(1)
        quant_w(1)
        row_sums(1)
        mix(1)
        finish(1)
